import numpy as np
import ml_dtypes


def mxq(x, axis, fmt="e4m3"):
    dtype, down = {"e4m3": (ml_dtypes.float8_e4m3fn, 7), "e5m2": (ml_dtypes.float8_e5m2, 14)}[fmt]
    v = np.moveaxis(np.asarray(x, np.float32).astype(ml_dtypes.bfloat16).astype(np.float64), axis, -1)
    blocks = v.reshape(v.shape[:-1] + (-1, 32))
    amax = np.abs(blocks).max(-1, keepdims=True)
    byte = np.maximum(np.where(amax > 0, np.frexp(amax)[1] - 1 + 127, 0) - down, 1)
    scale = np.exp2(byte - 127.0)
    codes = (blocks / scale).astype(np.float32).astype(dtype).astype(np.float64)
    return np.moveaxis((codes * scale).reshape(v.shape), -1, axis)


WIDE = False


def mx_kscale(k):
    if not WIDE:
        return np.ones(k)
    levels = np.array([10, -10, 5, -5, 0])
    if k % 512:
        return np.exp2(np.random.permutation(np.resize(levels, k // 32))).repeat(32)
    a = np.empty((k // 512, 16))
    for p in range(k // 512):
        a[p, :8] = np.random.permutation(np.resize(levels, 8))
        for g in range(8):
            far = levels[np.abs(levels - a[p, g]) >= 10]
            a[p, g + 8] = far[np.random.randint(len(far))]
    return np.exp2(a.ravel()).repeat(32)


def f64(x):
    return np.asarray(x).astype(np.float64)


def striped(idx):
    return np.tile(idx.reshape(-1, 16).T, (8, 1)).astype(np.uint16)


def unstriped(offs):
    return offs[:16].T.reshape(-1).astype(np.int64)


def gelu(v):
    return 0.5 * v * (1.0 + np.tanh(np.sqrt(2.0 / np.pi) * (v + 0.044715 * v**3)))


K, T, N = 1024, 512, 128


def setup_inputs():
    n = np.random.standard_normal
    s = mx_kscale(K)[:, None]
    idx = np.random.permutation(K)
    x = n((T, K))
    x[:, idx] *= s[:, 0]
    return {
        "x": x.astype(np.float32),
        "w": (n((K, N)) / np.sqrt(K) / s).astype(np.float32),
        "b": (0.3 * n((N, 1))).astype(np.float32),
        "offs": striped(idx),
    }


def reference(x, w, b, offs):
    idx = unstriped(offs)
    xq = mxq(f64(x)[:, idx], 1, "e4m3").T
    return gelu((mxq(f64(w), 0, "e4m3").T @ xq) + f64(b))

@@ -1,0 +1,166 @@
+from contextlib import ExitStack
+
+import concourse.mybir as mybir
+from concourse.masks import make_identity
+
+T, K, N = 512, 1024, 128
+FLOPS = 2 * T * K * N
+
+F32 = mybir.dt.float32
+BF16 = mybir.dt.bfloat16
+U32 = mybir.dt.uint32
+U16 = mybir.dt.uint16
+U8 = mybir.dt.uint8
+FP8X4 = mybir.dt.float8_e4m3fn_x4
+GELU = mybir.ActivationFunctionType.Gelu_apprx_tanh
+
+P = 128
+PACK = 4
+K_PASS = P * PACK
+PASSES = K // K_PASS
+GROUP = 2 * P
+GROUPS = T // GROUP
+HALF = K // 2
+
+
+def tile_picked_actorder_lin_gelu_perm_l_kernel(tc, x, w, b, offs, out):
+    nc = tc.nc
+    with ExitStack() as ctx:
+        lists = ctx.enter_context(tc.tile_pool(name="lists", bufs=1))
+        keep = ctx.enter_context(tc.tile_pool(name="keep", bufs=1))
+        psum = ctx.enter_context(tc.psum_pool(name="psum", bufs=1))
+
+        offsets = lists.tile([P, K // 16], U16, name="offsets")
+
+        raw = [[keep.tile([P, 2, HALF], F32, name=f"raw{u}{h}") for h in range(2)] for u in range(GROUPS)]
+        bias = keep.tile([P, 1], F32, name="bias")
+        w_raw = keep.tile([P, PASSES, PACK, N], F32, name="w_raw")
+
+        def load_x(u, h):
+            nc.sync.dma_start(
+                out=raw[u][h][:],
+                in_=x[u * GROUP : (u + 1) * GROUP, h * HALF : (h + 1) * HALF].rearrange("(p e) c -> p e c", e=2),
+            )
+
+        load_x(0, 0)
+        nc.sync.dma_start(offsets[:], offs)
+        load_x(0, 1)
+        load_x(1, 0)
+        load_x(1, 1)
+        for g in range(PASSES):
+            nc.sync.dma_start(
+                out=w_raw[:, g, :, :],
+                in_=w[g * K_PASS : (g + 1) * K_PASS, :].rearrange("(p j) m -> p j m", j=PACK),
+            )
+        nc.scalar.dma_start(out=bias[:], in_=b)
+
+        ident = keep.tile([P, P], F32, name="ident")
+        make_identity(nc, ident[:])
+        warm = keep.tile([P, 1], F32, name="warm")
+        nc.vector.memset(warm[:], 0.0)
+        warm_out = keep.tile([P, 1], F32, name="warm_out")
+        nc.scalar.activation(warm_out[:], warm[:], GELU)
+
+        win = [keep.tile([P, 2 * K], BF16, name=f"win{u}", align_bytes=64) for u in range(GROUPS)]
+
+        def cast(copy, u, c0, c1):
+            h = c0 // HALF
+            copy(
+                out=win[u][:, 2 * c0 : 2 * c1].rearrange("p (c e) -> p c e", e=2),
+                in_=raw[u][h][:, :, c0 - h * HALF : c1 - h * HALF].rearrange("p e c -> p c e"),
+            )
+
+        gathered = [[keep.tile([P, 2 * K_PASS], BF16, name=f"gat{u}{g}", align_bytes=64) for g in range(PASSES)] for u in range(GROUPS)]
+
+        def gather(u, g):
+            nc.vector.tensor_copy(
+                gathered[u][g][:].bitcast(U32).rearrange("p (t m) -> p m t", t=PACK),
+                win[u][:].bitcast(U32).indirect(offsets[:, g * (K_PASS // 16) : (g + 1) * (K_PASS // 16)]),
+            )
+
+        turned = [[psum.tile([P, PACK, P], F32, name=f"turned{u}{g}") for g in range(PASSES)] for u in range(GROUPS)]
+
+        last_bank = psum.tile([P, PACK, P], F32, name="last_bank")
+
+        def turn(u, g, bank=None):
+            bank = turned[u][g] if bank is None else bank
+            for t in range(PACK):
+                nc.tensor.transpose(
+                    bank[:, t, :], gathered[u][g][:].bitcast(F32)[:, t * P : (t + 1) * P], ident[:]
+                )
+
+        grouped = [[keep.tile([P, GROUP, PACK], BF16, name=f"grp{u}{g}", align_bytes=64) for g in range(PASSES)] for u in range(GROUPS)]
+        codes = [[keep.tile([P, GROUP], U32, name=f"codes{u}{g}", align_bytes=64) for g in range(PASSES)] for u in range(GROUPS)]
+        scales = [[keep.tile([P, GROUP], U8, name=f"scales{u}{g}", align_bytes=64) for g in range(PASSES)] for u in range(GROUPS)]
+
+        def lay(copy, u, g, r0=0, r1=GROUP, bank=None):
+            bank = turned[u][g] if bank is None else bank
+            copy(
+                out=grouped[u][g][:, r0:r1, :],
+                in_=bank[:].rearrange("p t q -> p (t q)").bitcast(BF16).rearrange("p (t r) -> p r t", t=PACK)[:, r0:r1, :],
+            )
+
+        def quantize(u, g):
+            nc.vector.quantize_mx(
+                out=codes[u][g][:].bitcast(FP8X4),
+                scales=scales[u][g][:],
+                in_=grouped[u][g][:].rearrange("p r t -> p (r t)"),
+            )
+
+        w_grouped = keep.tile([P, PASSES, N, PACK], BF16, name="w_grouped", align_bytes=64)
+        w_codes = keep.tile([P, PASSES * N], U32, name="w_codes", align_bytes=64)
+        w_scales = keep.tile([P, PASSES * N], U8, name="w_scales", align_bytes=64)
+
+        V, S, G = nc.vector.tensor_copy, nc.scalar.copy, nc.gpsimd.tensor_copy
+        cast(V, 0, 0, HALF)
+        cast(V, 0, 512, 792)
+        cast(S, 0, 792, 936)
+        cast(G, 0, 936, 1024)
+        gather(0, 0)
+        cast(S, 1, 0, 256)
+        cast(G, 1, 256, 512)
+        turn(0, 0)
+        cast(S, 1, 512, 768)
+        cast(G, 1, 768, 1024)
+        gather(0, 1)
+        turn(0, 1)
+        lay(S, 0, 0)
+        gather(1, 0)
+        turn(1, 0)
+        for g in range(PASSES):
+            G(out=w_grouped[:, g, :, :], in_=w_raw[:, g, :, :].rearrange("p j m -> p m j"))
+        quantize(0, 0)
+        lay(S, 0, 1)
+        gather(1, 1)
+        turn(1, 1)
+        turn(1, 1, last_bank)
+        nc.vector.quantize_mx(
+            out=w_codes[:].bitcast(FP8X4),
+            scales=w_scales[:],
+            in_=w_grouped[:].rearrange("p g m j -> p (g m j)"),
+        )
+        quantize(0, 1)
+        lay(S, 1, 0)
+
+        def product(u):
+            acc = psum.tile([N, GROUP], F32, name=f"acc{u}")
+            for g in range(PASSES):
+                nc.tensor.matmul_mx(
+                    out=acc[:],
+                    lhsT=w_codes[:, g * N : (g + 1) * N].bitcast(FP8X4),
+                    lhsT_scale=w_scales[:, g * N : (g + 1) * N],
+                    rhs=codes[u][g][:].bitcast(FP8X4),
+                    rhs_scale=scales[u][g][:],
+                    start=(g == 0),
+                    stop=(g == PASSES - 1),
+                )
+            result = keep.tile([N, GROUP], F32, name=f"result{u}")
+            nc.scalar.activation(result[:], acc[:], GELU, bias=bias[:])
+            nc.sync.dma_start(out=out[:, u * GROUP : (u + 1) * GROUP], in_=result[:])
+
+        lay(S, 1, 1, 0, 128)
+        quantize(1, 0)
+        product(0)
+        lay(V, 1, 1, 128, 256, last_bank)
+        quantize(1, 1)
+        product(1)

@@ -111,24 +111,31 @@ def tile_picked_actorder_lin_gelu_perm_l_kernel(tc, x, w, b, offs, out):
         w_codes = keep.tile([P, PASSES * N], U32, name="w_codes", align_bytes=64)
         w_scales = keep.tile([P, PASSES * N], U8, name="w_scales", align_bytes=64)
 
-        V, S, G = nc.vector.tensor_copy, nc.scalar.copy, nc.gpsimd.tensor_copy
+        V, S = nc.vector.tensor_copy, nc.scalar.copy
+
+        def G(out, in_):
+            nc.gpsimd.tensor_scalar(out, in_, 1.0, 0.0, mybir.AluOpType.mult, mybir.AluOpType.add)
+
         cast(V, 0, 0, HALF)
-        cast(V, 0, 512, 792)
-        cast(S, 0, 792, 936)
-        cast(G, 0, 936, 1024)
+        cast(V, 0, 512, 832)
+        cast(S, 0, 832, 1024)
         gather(0, 0)
         cast(S, 1, 0, 256)
         cast(G, 1, 256, 512)
         turn(0, 0)
-        cast(S, 1, 512, 768)
-        cast(G, 1, 768, 1024)
+        cast(S, 1, 512, 800)
+        cast(G, 1, 800, 1024)
         gather(0, 1)
         turn(0, 1)
         lay(S, 0, 0)
         gather(1, 0)
         turn(1, 0)
         for g in range(PASSES):
-            G(out=w_grouped[:, g, :, :], in_=w_raw[:, g, :, :].rearrange("p j m -> p m j"))
+            for m0 in range(0, N, 64):
+                G(
+                    out=w_grouped[:, g, m0 : m0 + 64, :],
+                    in_=w_raw[:, g, :, m0 : m0 + 64].rearrange("p j m -> p m j"),
+                )
         quantize(0, 0)
         lay(S, 0, 1)
         gather(1, 1)

from contextlib import ExitStack

import concourse.mybir as mybir
from concourse.masks import make_identity

T, K, N = 512, 1024, 128
FLOPS = 2 * T * K * N

F32 = mybir.dt.float32
BF16 = mybir.dt.bfloat16
U32 = mybir.dt.uint32
U16 = mybir.dt.uint16
U8 = mybir.dt.uint8
FP8X4 = mybir.dt.float8_e4m3fn_x4
GELU = mybir.ActivationFunctionType.Gelu_apprx_tanh

P = 128
PACK = 4
K_PASS = P * PACK
PASSES = K // K_PASS
GROUP = 2 * P
GROUPS = T // GROUP
HALF = K // 2


def tile_picked_actorder_lin_gelu_perm_l_kernel(tc, x, w, b, offs, out):
    nc = tc.nc
    with ExitStack() as ctx:
        lists = ctx.enter_context(tc.tile_pool(name="lists", bufs=1))
        keep = ctx.enter_context(tc.tile_pool(name="keep", bufs=1))
        psum = ctx.enter_context(tc.psum_pool(name="psum", bufs=1))

        offsets = lists.tile([P, K // 16], U16, name="offsets")

        raw = [[keep.tile([P, 2, HALF], F32, name=f"raw{u}{h}") for h in range(2)] for u in range(GROUPS)]
        bias = keep.tile([P, 1], F32, name="bias")
        w_raw = keep.tile([P, PASSES, PACK, N], F32, name="w_raw")

        def load_x(u, h):
            nc.sync.dma_start(
                out=raw[u][h][:],
                in_=x[u * GROUP : (u + 1) * GROUP, h * HALF : (h + 1) * HALF].rearrange("(p e) c -> p e c", e=2),
            )

        load_x(0, 0)
        nc.sync.dma_start(offsets[:], offs)
        load_x(0, 1)
        load_x(1, 0)
        load_x(1, 1)
        for g in range(PASSES):
            nc.sync.dma_start(
                out=w_raw[:, g, :, :],
                in_=w[g * K_PASS : (g + 1) * K_PASS, :].rearrange("(p j) m -> p j m", j=PACK),
            )
        nc.scalar.dma_start(out=bias[:], in_=b)

        ident = keep.tile([P, P], F32, name="ident")
        make_identity(nc, ident[:])
        warm = keep.tile([P, 1], F32, name="warm")
        nc.vector.memset(warm[:], 0.0)
        warm_out = keep.tile([P, 1], F32, name="warm_out")
        nc.scalar.activation(warm_out[:], warm[:], GELU)

        win = [keep.tile([P, 2 * K], BF16, name=f"win{u}", align_bytes=64) for u in range(GROUPS)]

        def cast(copy, u, c0, c1):
            h = c0 // HALF
            copy(
                out=win[u][:, 2 * c0 : 2 * c1].rearrange("p (c e) -> p c e", e=2),
                in_=raw[u][h][:, :, c0 - h * HALF : c1 - h * HALF].rearrange("p e c -> p c e"),
            )

        gathered = [[keep.tile([P, 2 * K_PASS], BF16, name=f"gat{u}{g}", align_bytes=64) for g in range(PASSES)] for u in range(GROUPS)]

        def gather(u, g):
            nc.vector.tensor_copy(
                gathered[u][g][:].bitcast(U32).rearrange("p (t m) -> p m t", t=PACK),
                win[u][:].bitcast(U32).indirect(offsets[:, g * (K_PASS // 16) : (g + 1) * (K_PASS // 16)]),
            )

        turned = [[psum.tile([P, PACK, P], F32, name=f"turned{u}{g}") for g in range(PASSES)] for u in range(GROUPS)]

        last_bank = psum.tile([P, PACK, P], F32, name="last_bank")

        def turn(u, g, bank=None):
            bank = turned[u][g] if bank is None else bank
            for t in range(PACK):
                nc.tensor.transpose(
                    bank[:, t, :], gathered[u][g][:].bitcast(F32)[:, t * P : (t + 1) * P], ident[:]
                )

        grouped = [[keep.tile([P, GROUP, PACK], BF16, name=f"grp{u}{g}", align_bytes=64) for g in range(PASSES)] for u in range(GROUPS)]
        codes = [[keep.tile([P, GROUP], U32, name=f"codes{u}{g}", align_bytes=64) for g in range(PASSES)] for u in range(GROUPS)]
        scales = [[keep.tile([P, GROUP], U8, name=f"scales{u}{g}", align_bytes=64) for g in range(PASSES)] for u in range(GROUPS)]

        def lay(copy, u, g, r0=0, r1=GROUP, bank=None):
            bank = turned[u][g] if bank is None else bank
            copy(
                out=grouped[u][g][:, r0:r1, :],
                in_=bank[:].rearrange("p t q -> p (t q)").bitcast(BF16).rearrange("p (t r) -> p r t", t=PACK)[:, r0:r1, :],
            )

        def quantize(u, g):
            nc.vector.quantize_mx(
                out=codes[u][g][:].bitcast(FP8X4),
                scales=scales[u][g][:],
                in_=grouped[u][g][:].rearrange("p r t -> p (r t)"),
            )

        w_grouped = keep.tile([P, PASSES, N, PACK], BF16, name="w_grouped", align_bytes=64)
        w_codes = keep.tile([P, PASSES * N], U32, name="w_codes", align_bytes=64)
        w_scales = keep.tile([P, PASSES * N], U8, name="w_scales", align_bytes=64)

        V, S = nc.vector.tensor_copy, nc.scalar.copy

        def G(out, in_):
            nc.gpsimd.tensor_scalar(out, in_, 1.0, 0.0, mybir.AluOpType.mult, mybir.AluOpType.add)

        cast(V, 0, 0, HALF)
        cast(V, 0, 512, 832)
        cast(S, 0, 832, 1024)
        gather(0, 0)
        cast(S, 1, 0, 256)
        cast(G, 1, 256, 512)
        turn(0, 0)
        cast(S, 1, 512, 800)
        cast(G, 1, 800, 1024)
        gather(0, 1)
        turn(0, 1)
        lay(S, 0, 0)
        gather(1, 0)
        turn(1, 0)
        for g in range(PASSES):
            for m0 in range(0, N, 64):
                G(
                    out=w_grouped[:, g, m0 : m0 + 64, :],
                    in_=w_raw[:, g, :, m0 : m0 + 64].rearrange("p j m -> p m j"),
                )
        quantize(0, 0)
        lay(S, 0, 1)
        gather(1, 1)
        turn(1, 1)
        turn(1, 1, last_bank)
        nc.vector.quantize_mx(
            out=w_codes[:].bitcast(FP8X4),
            scales=w_scales[:],
            in_=w_grouped[:].rearrange("p g m j -> p (g m j)"),
        )
        quantize(0, 1)
        lay(S, 1, 0)

        def product(u):
            acc = psum.tile([N, GROUP], F32, name=f"acc{u}")
            for g in range(PASSES):
                nc.tensor.matmul_mx(
                    out=acc[:],
                    lhsT=w_codes[:, g * N : (g + 1) * N].bitcast(FP8X4),
                    lhsT_scale=w_scales[:, g * N : (g + 1) * N],
                    rhs=codes[u][g][:].bitcast(FP8X4),
                    rhs_scale=scales[u][g][:],
                    start=(g == 0),
                    stop=(g == PASSES - 1),
                )
            result = keep.tile([N, GROUP], F32, name=f"result{u}")
            nc.scalar.activation(result[:], acc[:], GELU, bias=bias[:])
            nc.sync.dma_start(out=out[:, u * GROUP : (u + 1) * GROUP], in_=result[:])

        lay(S, 1, 1, 0, 128)
        quantize(1, 0)
        product(0)
        lay(V, 1, 1, 128, 256, last_bank)
        quantize(1, 1)
        product(1)
